import numpy as np
import ml_dtypes


def mxq(x, axis, fmt="e4m3"):
    dtype, down = {"e4m3": (ml_dtypes.float8_e4m3fn, 7), "e5m2": (ml_dtypes.float8_e5m2, 14)}[fmt]
    v = np.moveaxis(np.asarray(x, np.float32).astype(ml_dtypes.bfloat16).astype(np.float64), axis, -1)
    blocks = v.reshape(v.shape[:-1] + (-1, 32))
    amax = np.abs(blocks).max(-1, keepdims=True)
    byte = np.maximum(np.where(amax > 0, np.frexp(amax)[1] - 1 + 127, 0) - down, 1)
    scale = np.exp2(byte - 127.0)
    codes = (blocks / scale).astype(np.float32).astype(dtype).astype(np.float64)
    return np.moveaxis((codes * scale).reshape(v.shape), -1, axis)


WIDE = False


def mx_kscale(k):
    if not WIDE:
        return np.ones(k)
    levels = np.array([30, -30])
    if k % 512:
        return np.exp2(np.random.permutation(np.resize(levels, k // 32))).repeat(32)
    a = np.empty((k // 512, 16))
    for p in range(k // 512):
        a[p, :8] = np.random.permutation(np.resize(levels, 8))
        for g in range(8):
            far = levels[np.abs(levels - a[p, g]) >= 10]
            a[p, g + 8] = far[np.random.randint(len(far))]
    return np.exp2(a.ravel()).repeat(32)


def f64(x):
    return np.asarray(x).astype(np.float64)


def striped(idx):
    return np.tile(np.asarray(idx).reshape(-1, 16).T, (8, 1)).astype(np.uint16)


def unstriped(offs):
    return offs[:16].T.reshape(-1).astype(np.int64)


E2M1 = np.array([0.0, 0.5, 1.0, 1.5, 2.0, 3.0, 4.0, 6.0, -0.0, -0.5, -1.0, -1.5, -2.0, -3.0, -4.0, -6.0])


def pack_weight(w, fmt):
    k, n = w.shape
    w = f64(np.asarray(w, np.float32).astype(ml_dtypes.bfloat16)).reshape(k // 32, 32, n)
    amax = np.abs(w).max(1)
    if fmt in ("e4m3", "e5m2"):
        byte = np.frexp(amax)[1] - 1 + 127 - (7 if fmt == "e4m3" else 14)
    else:
        mant, ex = np.frexp(amax / 6.0)
        byte = np.where(mant > 0.5, ex, ex - 1) + 127
    byte = np.clip(np.where(amax > 0, byte, 1), 1, 254)
    scaled = (w * np.exp2(127.0 - byte)[:, None, :]).reshape(k, n).astype(np.float32)
    by_word = np.ascontiguousarray(scaled.reshape(k // 512, 128, 4, n).transpose(0, 1, 3, 2))
    if fmt in ("e4m3", "e5m2"):
        words = by_word.astype(ml_dtypes.float8_e4m3fn if fmt == "e4m3" else ml_dtypes.float8_e5m2).view(np.uint8)
    else:
        c = by_word.astype(ml_dtypes.float4_e2m1fn).view(np.uint8) & 0xF
        words = (c[..., 0::2] | (c[..., 1::2] << 4)).reshape(k // 512, 128, 2 * n)
    return np.ascontiguousarray(words), np.ascontiguousarray(byte.astype(np.uint8).reshape(k // 512, 16, n))


def unpack_weight(words, scales, fmt):
    g, _, n = scales.shape
    words = np.ascontiguousarray(words).reshape(g, 128, n, -1)
    if fmt in ("e4m3", "e5m2"):
        vals = words.view(ml_dtypes.float8_e4m3fn if fmt == "e4m3" else ml_dtypes.float8_e5m2).astype(np.float64)
    else:
        nib = np.empty((g, 128, n, 4), np.uint8)
        nib[..., 0::2] = words & 0xF
        nib[..., 1::2] = words >> 4
        vals = E2M1[nib]
    vals = vals * np.repeat(np.exp2(scales.astype(np.float64) - 127.0), 8, axis=1)[..., None]
    return vals.transpose(0, 1, 3, 2).reshape(g * 512, n)


K, T, J, I, R, G = 512, 512, 256, 256, 512, 32


def setup_inputs():
    n = np.random.standard_normal
    idx = np.random.permutation(T)[:J]
    idx2 = np.random.permutation(T)[:I]
    fk = mx_kscale(K)
    fr = mx_kscale(R)
    xtp = pack_weight(n((K, T)) / fk[:, None], "e2m1")
    wap = pack_weight(n((K, R)) * 0.5 / np.sqrt(K) * fk[:, None] * fr, "e5m2")
    wbp = pack_weight(n((K, R)) * 1 / np.sqrt(K) * fk[:, None] / fr, "e4m3")
    return {
        "xt_words": xtp[0],
        "xt_scales": xtp[1],
        "wa_words": wap[0],
        "wa_scales": wap[1],
        "wb_words": wbp[0],
        "wb_scales": wbp[1],
        "offs": striped(idx),
        "offs2": striped(idx2),
    }


def reference(xt_words, xt_scales, wa_words, wa_scales, wb_words, wb_scales, offs, offs2):
    idx = unstriped(offs)
    idx2 = unstriped(offs2)
    xtu = unpack_weight(xt_words, xt_scales, "e2m1")
    wau = unpack_weight(wa_words, wa_scales, "e5m2")
    wbu = unpack_weight(wb_words, wb_scales, "e4m3")
    xtidxg = xtu[:, idx]
    za = wau.T @ xtidxg
    ha = np.maximum(za, 0.0)
    xtidx2g = xtu[:, idx2]
    zb = wbu.T @ xtidx2g
    mb1 = zb.reshape(R, G, I // G).mean(axis=2)
    mb2 = np.repeat(mb1, I // G, axis=1)
    hb = zb - mb2
    haq = mxq(ha, 0, "e5m2")
    hbq = mxq(hb, 0, "e5m2")
    a0 = haq.T @ hbq
    a1 = np.pad(a0, ((0, 0), (1, 0)))[:, :I]
    y = 0.04 * np.abs(a0 - a1)
    return y

@@ -1,0 +1,170 @@
+from contextlib import ExitStack
+
+import concourse.mybir as mybir
+
+K, T, J, I, R, G = 512, 512, 256, 256, 512, 32
+FLOPS = 2 * K * R * J + 2 * K * R * I + 2 * R * J * I
+
+F32 = mybir.dt.float32
+BF16 = mybir.dt.bfloat16
+I32 = mybir.dt.int32
+U32 = mybir.dt.uint32
+U16 = mybir.dt.uint16
+U8 = mybir.dt.uint8
+E2M1 = mybir.dt.float4_e2m1fn_x4
+E4M3 = mybir.dt.float8_e4m3fn_x4
+E5M2 = mybir.dt.float8_e5m2_x4
+ALU = mybir.AluOpType
+ACT = mybir.ActivationFunctionType
+
+P = 128
+PACK = 4
+HALF = 128
+BUNDLE = 8
+LEAD = 4
+
+
+def load_scale_rows(queues, plane, scales):
+    rows = scales[0].bitcast(I32)
+    for q in range(4):
+        queues[q].dma_start(out=plane[:].bitcast(I32)[32 * q : 32 * q + 4, :], in_=rows[4 * q : 4 * q + 4, :])
+
+
+def deal_weight(nc, dealt, raw, run):
+    nc.scalar.copy(
+        out=dealt.rearrange("p (t b u) -> p t b u", t=PACK, u=run),
+        in_=raw.rearrange("p (b t u) -> p t b u", t=PACK, u=run),
+    )
+
+
+def tile_list_meet_plain_levelled_steps_kernel(
+    tc, xt_words, xt_scales, wa_words, wa_scales, wb_words, wb_scales, offs, offs2, out
+):
+    nc = tc.nc
+    with ExitStack() as ctx:
+        sb = ctx.enter_context(tc.tile_pool(name="sb", bufs=1))
+        ps = ctx.enter_context(tc.psum_pool(name="ps", bufs=1))
+
+        rows_list = sb.tile([P, J // 16], U16, name="rows_list")
+        cols_list = sb.tile([P, I // 16], U16, name="cols_list")
+        x_words = sb.tile([P, T], U16, name="x_words", align_bytes=64)
+        x_plane = sb.tile([P, T], U8, name="x_plane", align_bytes=64)
+        wa_raw = sb.tile([P, R], U32, name="wa_raw", align_bytes=64)
+        wb_raw = sb.tile([P, R], U32, name="wb_raw", align_bytes=64)
+        wa_raw_plane = sb.tile([P, R], U8, name="wa_raw_plane", align_bytes=64)
+        wb_raw_plane = sb.tile([P, R], U8, name="wb_raw_plane", align_bytes=64)
+        wa = sb.tile([P, R], U32, name="wa", align_bytes=64)
+        wb = sb.tile([P, R], U32, name="wb", align_bytes=64)
+        wa_plane = sb.tile([P, R], U8, name="wa_plane", align_bytes=64)
+        wb_plane = sb.tile([P, R], U8, name="wb_plane", align_bytes=64)
+        scores = sb.tile([P, 2, LEAD + I], F32, name="scores", align_bytes=64)
+
+        nc.vector.memset(x_plane[:].bitcast(I32), 0)
+        nc.gpsimd.memset(wb_raw_plane[:].bitcast(I32), 0)
+        nc.gpsimd.memset(wa_raw_plane[:].bitcast(I32), 0)
+        nc.gpsimd.memset(scores[:, :, 0:LEAD], 0.0)
+
+        nc.sync.dma_start(out=x_words[:].bitcast(I32), in_=xt_words[0].bitcast(I32))
+        nc.sync.dma_start(cols_list[:], offs2)
+        nc.sync.dma_start(out=wb_raw[:].bitcast(I32), in_=wb_words[0].rearrange("p n t -> p (n t)").bitcast(I32))
+        load_scale_rows([nc.scalar] * 4, x_plane, xt_scales)
+        nc.sync.dma_start(rows_list[:], offs)
+        load_scale_rows([nc.sync] * 4, wb_raw_plane, wb_scales)
+        nc.sync.dma_start(out=wa_raw[:].bitcast(I32), in_=wa_words[0].rearrange("p n t -> p (n t)").bitcast(I32))
+        load_scale_rows([nc.gpsimd] + [nc.sync] * 3, wa_raw_plane, wa_scales)
+
+        deal_weight(nc, wb[:], wb_raw[:], 8)
+        deal_weight(nc, wb_plane[:].bitcast(U32), wb_raw_plane[:].bitcast(U32), 2)
+
+        def first_stage(bank, w, w_plane, fmt, words, plane):
+            for t in range(PACK):
+                cols = slice(t * P, (t + 1) * P)
+                nc.tensor.matmul_mx(
+                    out=bank[:, t, :],
+                    lhsT=w[:, cols].bitcast(fmt),
+                    lhsT_scale=w_plane[:, cols],
+                    rhs=words.bitcast(E2M1),
+                    rhs_scale=plane,
+                    start=True,
+                    stop=True,
+                )
+
+        zb = []
+        for h in range(2):
+            entries = cols_list[:, 8 * h : 8 * h + 8]
+            words = sb.tile([P, HALF], U16, name="xb_words%d" % h, align_bytes=64)
+            plane = sb.tile([P, HALF], U8, name="xb_plane%d" % h, align_bytes=64)
+            nc.vector.tensor_copy(words[:], x_words[:].indirect(entries))
+            nc.vector.tensor_copy(plane[:], x_plane[:].indirect(entries))
+            bank = ps.tile([P, PACK, HALF], F32, name="zb%d" % h)
+            first_stage(bank, wb, wb_plane, E4M3, words[:], plane[:])
+            zb.append(bank)
+
+        xa_words = sb.tile([P, J], U16, name="xa_words", align_bytes=64)
+        xa_plane = sb.tile([P, J], U8, name="xa_plane", align_bytes=64)
+        nc.vector.tensor_copy(xa_words[:], x_words[:].indirect(rows_list[:]))
+        nc.vector.tensor_copy(xa_plane[:], x_plane[:].indirect(rows_list[:]))
+
+        means = []
+        for h in range(2):
+            sums = sb.tile([P, HALF // BUNDLE, PACK], F32, name="sums%d" % h, align_bytes=64)
+            nc.vector.tensor_reduce(
+                out=sums[:],
+                in_=zb[h][:].rearrange("p t (g e) -> p g t e", e=BUNDLE),
+                axis=mybir.AxisListType.X,
+                op=ALU.add,
+            )
+            mean = sb.tile([P, HALF // BUNDLE, PACK], F32, name="mean%d" % h, align_bytes=64)
+            nc.gpsimd.tensor_scalar(mean[:], sums[:], 1.0 / BUNDLE, 0.0, ALU.mult, ALU.add)
+            means.append(mean)
+
+        deal_weight(nc, wa[:], wa_raw[:], 8)
+        deal_weight(nc, wa_plane[:].bitcast(U32), wa_raw_plane[:].bitcast(U32), 2)
+        ha = sb.tile([P, J, PACK], BF16, name="ha", align_bytes=64)
+        for h in range(2):
+            cols = slice(h * HALF, (h + 1) * HALF)
+            bank = ps.tile([P, PACK, HALF], F32, name="za%d" % h)
+            first_stage(bank, wa, wa_plane, E5M2, xa_words[:, cols], xa_plane[:, cols])
+            nc.scalar.activation(ha[:, cols, :], bank[:].rearrange("p t n -> p n t"), ACT.Relu)
+
+        hb = []
+        for h in range(2):
+            centred = sb.tile([P, HALF, PACK], BF16, name="hb%d" % h, align_bytes=64)
+            nc.vector.tensor_tensor(
+                centred[:].rearrange("p (g e) t -> p g e t", e=BUNDLE),
+                zb[h][:].rearrange("p t (g e) -> p g e t", e=BUNDLE),
+                means[h][:].unsqueeze(2).to_broadcast([P, HALF // BUNDLE, BUNDLE, PACK]),
+                ALU.subtract,
+            )
+            hb.append(centred)
+
+        ha_words = sb.tile([P, J], U32, name="ha_words", align_bytes=64)
+        ha_plane = sb.tile([P, J], U8, name="ha_plane", align_bytes=64)
+        nc.vector.quantize_mx(out=ha_words[:].bitcast(E5M2), scales=ha_plane[:], in_=ha[:].rearrange("p n t -> p (n t)"))
+
+        out_view = out.rearrange("(a p) i -> p a i", p=P)
+        for h in range(2):
+            hb_words = sb.tile([P, HALF], U32, name="hb_words%d" % h, align_bytes=64)
+            hb_plane = sb.tile([P, HALF], U8, name="hb_plane%d" % h, align_bytes=64)
+            nc.vector.quantize_mx(
+                out=hb_words[:].bitcast(E5M2), scales=hb_plane[:], in_=hb[h][:].rearrange("p n t -> p (n t)")
+            )
+            bank = ps.tile([P, 2, HALF], F32, name="a0_%d" % h)
+            for a in range(2):
+                rows = slice(a * P, (a + 1) * P)
+                nc.tensor.matmul_mx(
+                    out=bank[:, a, :],
+                    lhsT=ha_words[:, rows].bitcast(E5M2),
+                    lhsT_scale=ha_plane[:, rows],
+                    rhs=hb_words[:].bitcast(E5M2),
+                    rhs_scale=hb_plane[:],
+                    start=True,
+                    stop=True,
+                )
+            first = LEAD + h * HALF
+            nc.scalar.copy(out=scores[:, :, first : first + HALF], in_=bank[:])
+            step = sb.tile([P, 2, HALF], F32, name="step%d" % h, align_bytes=64)
+            nc.vector.tensor_tensor(step[:], bank[:], scores[:, :, first - 1 : first - 1 + HALF], ALU.subtract)
+            result = sb.tile([P, 2, HALF], F32, name="result%d" % h, align_bytes=64)
+            nc.scalar.activation(result[:], step[:], ACT.Abs, scale=0.04)
+            nc.sync.dma_start(out=out_view[:, :, h * HALF : (h + 1) * HALF], in_=result[:])

@@ -59,19 +59,21 @@ def tile_list_meet_plain_levelled_steps_kernel(
         wb_plane = sb.tile([P, R], U8, name="wb_plane", align_bytes=64)
         scores = sb.tile([P, 2, LEAD + I], F32, name="scores", align_bytes=64)
 
-        nc.vector.memset(x_plane[:].bitcast(I32), 0)
+        zero = sb.tile([P, 2, 1], F32, name="zero", align_bytes=64)
+        nc.gpsimd.memset(x_plane[:].bitcast(I32), 0)
         nc.gpsimd.memset(wb_raw_plane[:].bitcast(I32), 0)
-        nc.gpsimd.memset(wa_raw_plane[:].bitcast(I32), 0)
-        nc.gpsimd.memset(scores[:, :, 0:LEAD], 0.0)
+        nc.gpsimd.memset(zero[:], 0.0)
+        nc.vector.memset(wa_raw_plane[:].bitcast(I32), 0)
 
-        nc.sync.dma_start(out=x_words[:].bitcast(I32), in_=xt_words[0].bitcast(I32))
         nc.sync.dma_start(cols_list[:], offs2)
+        nc.sync.dma_start(rows_list[:], offs)
+        nc.sync.dma_start(out=x_words[:].bitcast(I32), in_=xt_words[0].bitcast(I32))
         nc.sync.dma_start(out=wb_raw[:].bitcast(I32), in_=wb_words[0].rearrange("p n t -> p (n t)").bitcast(I32))
         load_scale_rows([nc.scalar] * 4, x_plane, xt_scales)
-        nc.sync.dma_start(rows_list[:], offs)
-        load_scale_rows([nc.sync] * 4, wb_raw_plane, wb_scales)
+        nc.scalar.activation(scores[:, :, LEAD - 1 : LEAD], zero[:], ACT.Copy)
+        load_scale_rows([nc.gpsimd, nc.gpsimd, nc.sync, nc.sync], wb_raw_plane, wb_scales)
         nc.sync.dma_start(out=wa_raw[:].bitcast(I32), in_=wa_words[0].rearrange("p n t -> p (n t)").bitcast(I32))
-        load_scale_rows([nc.gpsimd] + [nc.sync] * 3, wa_raw_plane, wa_scales)
+        load_scale_rows([nc.sync] * 4, wa_raw_plane, wa_scales)
 
         deal_weight(nc, wb[:], wb_raw[:], 8)
         deal_weight(nc, wb_plane[:].bitcast(U32), wb_raw_plane[:].bitcast(U32), 2)
@@ -120,12 +122,14 @@ def tile_list_meet_plain_levelled_steps_kernel(
 
         deal_weight(nc, wa[:], wa_raw[:], 8)
         deal_weight(nc, wa_plane[:].bitcast(U32), wa_raw_plane[:].bitcast(U32), 2)
-        ha = sb.tile([P, J, PACK], BF16, name="ha", align_bytes=64)
+        ha = []
         for h in range(2):
             cols = slice(h * HALF, (h + 1) * HALF)
             bank = ps.tile([P, PACK, HALF], F32, name="za%d" % h)
             first_stage(bank, wa, wa_plane, E5M2, xa_words[:, cols], xa_plane[:, cols])
-            nc.scalar.activation(ha[:, cols, :], bank[:].rearrange("p t n -> p n t"), ACT.Relu)
+            kept = sb.tile([P, HALF, PACK], BF16, name="ha%d" % h, align_bytes=64)
+            nc.scalar.activation(kept[:], bank[:].rearrange("p t n -> p n t"), ACT.Relu)
+            ha.append(kept)
 
         hb = []
         for h in range(2):
@@ -138,33 +142,32 @@ def tile_list_meet_plain_levelled_steps_kernel(
             )
             hb.append(centred)
 
-        ha_words = sb.tile([P, J], U32, name="ha_words", align_bytes=64)
-        ha_plane = sb.tile([P, J], U8, name="ha_plane", align_bytes=64)
-        nc.vector.quantize_mx(out=ha_words[:].bitcast(E5M2), scales=ha_plane[:], in_=ha[:].rearrange("p n t -> p (n t)"))
+        def quantise(name, values):
+            words = sb.tile([P, HALF], U32, name=name + "_words", align_bytes=64)
+            plane = sb.tile([P, HALF], U8, name=name + "_plane", align_bytes=64)
+            nc.vector.quantize_mx(out=words[:].bitcast(E5M2), scales=plane[:], in_=values[:].rearrange("p n t -> p (n t)"))
+            return words, plane
 
-        out_view = out.rearrange("(a p) i -> p a i", p=P)
-        for h in range(2):
-            hb_words = sb.tile([P, HALF], U32, name="hb_words%d" % h, align_bytes=64)
-            hb_plane = sb.tile([P, HALF], U8, name="hb_plane%d" % h, align_bytes=64)
-            nc.vector.quantize_mx(
-                out=hb_words[:].bitcast(E5M2), scales=hb_plane[:], in_=hb[h][:].rearrange("p n t -> p (n t)")
-            )
-            bank = ps.tile([P, 2, HALF], F32, name="a0_%d" % h)
-            for a in range(2):
-                rows = slice(a * P, (a + 1) * P)
+        haq0 = quantise("ha0", ha[0])
+        hbq = [quantise("hb0", hb[0]), quantise("hb1", hb[1])]
+        haq = [haq0, quantise("ha1", ha[1])]
+
+        for a in range(2):
+            for h in range(2):
+                bank = ps.tile([P, HALF], F32, name="a0_%d%d" % (a, h))
                 nc.tensor.matmul_mx(
-                    out=bank[:, a, :],
-                    lhsT=ha_words[:, rows].bitcast(E5M2),
-                    lhsT_scale=ha_plane[:, rows],
-                    rhs=hb_words[:].bitcast(E5M2),
-                    rhs_scale=hb_plane[:],
+                    out=bank[:],
+                    lhsT=haq[a][0][:].bitcast(E5M2),
+                    lhsT_scale=haq[a][1][:],
+                    rhs=hbq[h][0][:].bitcast(E5M2),
+                    rhs_scale=hbq[h][1][:],
                     start=True,
                     stop=True,
                 )
-            first = LEAD + h * HALF
-            nc.scalar.copy(out=scores[:, :, first : first + HALF], in_=bank[:])
-            step = sb.tile([P, 2, HALF], F32, name="step%d" % h, align_bytes=64)
-            nc.vector.tensor_tensor(step[:], bank[:], scores[:, :, first - 1 : first - 1 + HALF], ALU.subtract)
-            result = sb.tile([P, 2, HALF], F32, name="result%d" % h, align_bytes=64)
-            nc.scalar.activation(result[:], step[:], ACT.Abs, scale=0.04)
-            nc.sync.dma_start(out=out_view[:, :, h * HALF : (h + 1) * HALF], in_=result[:])
+                first = LEAD + h * HALF
+                nc.scalar.copy(out=scores[:, a, first : first + HALF], in_=bank[:])
+                step = sb.tile([P, HALF], F32, name="step%d%d" % (a, h), align_bytes=64)
+                nc.vector.tensor_tensor(step[:], bank[:], scores[:, a, first - 1 : first - 1 + HALF], ALU.subtract)
+                result = sb.tile([P, HALF], F32, name="result%d%d" % (a, h), align_bytes=64)
+                nc.scalar.activation(result[:], step[:], ACT.Abs, scale=0.04)
+                nc.sync.dma_start(out=out[a * P : (a + 1) * P, h * HALF : (h + 1) * HALF], in_=result[:])

@@ -71,7 +71,7 @@ def tile_list_meet_plain_levelled_steps_kernel(
         nc.sync.dma_start(out=wb_raw[:].bitcast(I32), in_=wb_words[0].rearrange("p n t -> p (n t)").bitcast(I32))
         load_scale_rows([nc.scalar] * 4, x_plane, xt_scales)
         nc.scalar.activation(scores[:, :, LEAD - 1 : LEAD], zero[:], ACT.Copy)
-        load_scale_rows([nc.gpsimd, nc.gpsimd, nc.sync, nc.sync], wb_raw_plane, wb_scales)
+        load_scale_rows([nc.gpsimd, nc.sync, nc.sync, nc.sync], wb_raw_plane, wb_scales)
         nc.sync.dma_start(out=wa_raw[:].bitcast(I32), in_=wa_words[0].rearrange("p n t -> p (n t)").bitcast(I32))
         load_scale_rows([nc.sync] * 4, wa_raw_plane, wa_scales)
 

@@ -2,7 +2,7 @@ from contextlib import ExitStack
 
 import concourse.mybir as mybir
 
-K, T, J, I, R, G = 512, 512, 256, 256, 512, 32
+K, T, J, I, R = 512, 512, 256, 256, 512
 FLOPS = 2 * K * R * J + 2 * K * R * I + 2 * R * J * I
 
 F32 = mybir.dt.float32
@@ -19,22 +19,55 @@ ACT = mybir.ActivationFunctionType
 
 P = 128
 PACK = 4
+QUADRANTS = 4
+RUN = 8
+GROUP = 16
 HALF = 128
 BUNDLE = 8
 LEAD = 4
+FACTOR = 0.04
 
 
 def load_scale_rows(queues, plane, scales):
     rows = scales[0].bitcast(I32)
-    for q in range(4):
+    for q in range(QUADRANTS):
         queues[q].dma_start(out=plane[:].bitcast(I32)[32 * q : 32 * q + 4, :], in_=rows[4 * q : 4 * q + 4, :])
 
 
-def deal_weight(nc, dealt, raw, run):
-    nc.scalar.copy(
-        out=dealt.rearrange("p (t b u) -> p t b u", t=PACK, u=run),
-        in_=raw.rearrange("p (b t u) -> p t b u", t=PACK, u=run),
-    )
+def load_weight_words(nc, raw, words):
+    nc.sync.dma_start(out=raw[:].bitcast(I32), in_=words[0].rearrange("p n t -> p (n t)").bitcast(I32))
+
+
+def deal_weight(nc, words, plane, raw_words, raw_plane):
+    for dealt, raw, run in (
+        (words[:], raw_words[:], RUN),
+        (plane[:].bitcast(U32), raw_plane[:].bitcast(U32), RUN // 4),
+    ):
+        nc.scalar.copy(
+            out=dealt.rearrange("p (t b u) -> p t b u", t=PACK, u=run),
+            in_=raw.rearrange("p (b t u) -> p t b u", t=PACK, u=run),
+        )
+
+
+def first_stage(nc, bank, w_words, w_plane, w_format, picked_words, picked_plane):
+    for t in range(PACK):
+        cols = slice(t * P, (t + 1) * P)
+        nc.tensor.matmul_mx(
+            out=bank[:, t, :],
+            lhsT=w_words[:, cols].bitcast(w_format),
+            lhsT_scale=w_plane[:, cols],
+            rhs=picked_words.bitcast(E2M1),
+            rhs_scale=picked_plane,
+            start=True,
+            stop=True,
+        )
+
+
+def quantise(nc, pool, name, values):
+    words = pool.tile([P, HALF], U32, name=name + "_words", align_bytes=64)
+    plane = pool.tile([P, HALF], U8, name=name + "_plane", align_bytes=64)
+    nc.vector.quantize_mx(out=words[:].bitcast(E5M2), scales=plane[:], in_=values[:].rearrange("p n t -> p (n t)"))
+    return words, plane
 
 
 def tile_list_meet_plain_levelled_steps_kernel(
@@ -45,8 +78,8 @@ def tile_list_meet_plain_levelled_steps_kernel(
         sb = ctx.enter_context(tc.tile_pool(name="sb", bufs=1))
         ps = ctx.enter_context(tc.psum_pool(name="ps", bufs=1))
 
-        rows_list = sb.tile([P, J // 16], U16, name="rows_list")
-        cols_list = sb.tile([P, I // 16], U16, name="cols_list")
+        rows_list = sb.tile([P, J // GROUP], U16, name="rows_list")
+        cols_list = sb.tile([P, I // GROUP], U16, name="cols_list")
         x_words = sb.tile([P, T], U16, name="x_words", align_bytes=64)
         x_plane = sb.tile([P, T], U8, name="x_plane", align_bytes=64)
         wa_raw = sb.tile([P, R], U32, name="wa_raw", align_bytes=64)
@@ -66,41 +99,27 @@ def tile_list_meet_plain_levelled_steps_kernel(
         nc.vector.memset(wa_raw_plane[:].bitcast(I32), 0)
 
         nc.sync.dma_start(cols_list[:], offs2)
-        nc.sync.dma_start(rows_list[:], offs)
         nc.sync.dma_start(out=x_words[:].bitcast(I32), in_=xt_words[0].bitcast(I32))
-        nc.sync.dma_start(out=wb_raw[:].bitcast(I32), in_=wb_words[0].rearrange("p n t -> p (n t)").bitcast(I32))
-        load_scale_rows([nc.scalar] * 4, x_plane, xt_scales)
+        nc.sync.dma_start(rows_list[:], offs)
+        load_weight_words(nc, wb_raw, wb_words)
+        load_scale_rows([nc.scalar] * QUADRANTS, x_plane, xt_scales)
         nc.scalar.activation(scores[:, :, LEAD - 1 : LEAD], zero[:], ACT.Copy)
         load_scale_rows([nc.gpsimd, nc.sync, nc.sync, nc.sync], wb_raw_plane, wb_scales)
-        nc.sync.dma_start(out=wa_raw[:].bitcast(I32), in_=wa_words[0].rearrange("p n t -> p (n t)").bitcast(I32))
-        load_scale_rows([nc.sync] * 4, wa_raw_plane, wa_scales)
+        load_weight_words(nc, wa_raw, wa_words)
+        load_scale_rows([nc.sync] * QUADRANTS, wa_raw_plane, wa_scales)
 
-        deal_weight(nc, wb[:], wb_raw[:], 8)
-        deal_weight(nc, wb_plane[:].bitcast(U32), wb_raw_plane[:].bitcast(U32), 2)
-
-        def first_stage(bank, w, w_plane, fmt, words, plane):
-            for t in range(PACK):
-                cols = slice(t * P, (t + 1) * P)
-                nc.tensor.matmul_mx(
-                    out=bank[:, t, :],
-                    lhsT=w[:, cols].bitcast(fmt),
-                    lhsT_scale=w_plane[:, cols],
-                    rhs=words.bitcast(E2M1),
-                    rhs_scale=plane,
-                    start=True,
-                    stop=True,
-                )
+        deal_weight(nc, wb, wb_plane, wb_raw, wb_raw_plane)
 
         zb = []
         for h in range(2):
-            entries = cols_list[:, 8 * h : 8 * h + 8]
-            words = sb.tile([P, HALF], U16, name="xb_words%d" % h, align_bytes=64)
-            plane = sb.tile([P, HALF], U8, name="xb_plane%d" % h, align_bytes=64)
-            nc.vector.tensor_copy(words[:], x_words[:].indirect(entries))
-            nc.vector.tensor_copy(plane[:], x_plane[:].indirect(entries))
-            bank = ps.tile([P, PACK, HALF], F32, name="zb%d" % h)
-            first_stage(bank, wb, wb_plane, E4M3, words[:], plane[:])
-            zb.append(bank)
+            entries = cols_list[:, h * HALF // GROUP : (h + 1) * HALF // GROUP]
+            xb_words = sb.tile([P, HALF], U16, name="xb_words%d" % h, align_bytes=64)
+            xb_plane = sb.tile([P, HALF], U8, name="xb_plane%d" % h, align_bytes=64)
+            nc.vector.tensor_copy(xb_words[:], x_words[:].indirect(entries))
+            nc.vector.tensor_copy(xb_plane[:], x_plane[:].indirect(entries))
+            zb_half = ps.tile([P, PACK, HALF], F32, name="zb%d" % h)
+            first_stage(nc, zb_half, wb, wb_plane, E4M3, xb_words[:], xb_plane[:])
+            zb.append(zb_half)
 
         xa_words = sb.tile([P, J], U16, name="xa_words", align_bytes=64)
         xa_plane = sb.tile([P, J], U8, name="xa_plane", align_bytes=64)
@@ -120,43 +139,36 @@ def tile_list_meet_plain_levelled_steps_kernel(
             nc.gpsimd.tensor_scalar(mean[:], sums[:], 1.0 / BUNDLE, 0.0, ALU.mult, ALU.add)
             means.append(mean)
 
-        deal_weight(nc, wa[:], wa_raw[:], 8)
-        deal_weight(nc, wa_plane[:].bitcast(U32), wa_raw_plane[:].bitcast(U32), 2)
+        deal_weight(nc, wa, wa_plane, wa_raw, wa_raw_plane)
         ha = []
         for h in range(2):
             cols = slice(h * HALF, (h + 1) * HALF)
-            bank = ps.tile([P, PACK, HALF], F32, name="za%d" % h)
-            first_stage(bank, wa, wa_plane, E5M2, xa_words[:, cols], xa_plane[:, cols])
-            kept = sb.tile([P, HALF, PACK], BF16, name="ha%d" % h, align_bytes=64)
-            nc.scalar.activation(kept[:], bank[:].rearrange("p t n -> p n t"), ACT.Relu)
-            ha.append(kept)
+            za_half = ps.tile([P, PACK, HALF], F32, name="za%d" % h)
+            first_stage(nc, za_half, wa, wa_plane, E5M2, xa_words[:, cols], xa_plane[:, cols])
+            ha_half = sb.tile([P, HALF, PACK], BF16, name="ha%d" % h, align_bytes=64)
+            nc.scalar.activation(ha_half[:], za_half[:].rearrange("p t n -> p n t"), ACT.Relu)
+            ha.append(ha_half)
 
         hb = []
         for h in range(2):
-            centred = sb.tile([P, HALF, PACK], BF16, name="hb%d" % h, align_bytes=64)
+            hb_half = sb.tile([P, HALF, PACK], BF16, name="hb%d" % h, align_bytes=64)
             nc.vector.tensor_tensor(
-                centred[:].rearrange("p (g e) t -> p g e t", e=BUNDLE),
+                hb_half[:].rearrange("p (g e) t -> p g e t", e=BUNDLE),
                 zb[h][:].rearrange("p t (g e) -> p g e t", e=BUNDLE),
                 means[h][:].unsqueeze(2).to_broadcast([P, HALF // BUNDLE, BUNDLE, PACK]),
                 ALU.subtract,
             )
-            hb.append(centred)
+            hb.append(hb_half)
 
-        def quantise(name, values):
-            words = sb.tile([P, HALF], U32, name=name + "_words", align_bytes=64)
-            plane = sb.tile([P, HALF], U8, name=name + "_plane", align_bytes=64)
-            nc.vector.quantize_mx(out=words[:].bitcast(E5M2), scales=plane[:], in_=values[:].rearrange("p n t -> p (n t)"))
-            return words, plane
-
-        haq0 = quantise("ha0", ha[0])
-        hbq = [quantise("hb0", hb[0]), quantise("hb1", hb[1])]
-        haq = [haq0, quantise("ha1", ha[1])]
+        haq_first = quantise(nc, sb, "ha0", ha[0])
+        hbq = [quantise(nc, sb, "hb0", hb[0]), quantise(nc, sb, "hb1", hb[1])]
+        haq = [haq_first, quantise(nc, sb, "ha1", ha[1])]
 
         for a in range(2):
             for h in range(2):
-                bank = ps.tile([P, HALF], F32, name="a0_%d%d" % (a, h))
+                a0 = ps.tile([P, HALF], F32, name="a0_%d%d" % (a, h))
                 nc.tensor.matmul_mx(
-                    out=bank[:],
+                    out=a0[:],
                     lhsT=haq[a][0][:].bitcast(E5M2),
                     lhsT_scale=haq[a][1][:],
                     rhs=hbq[h][0][:].bitcast(E5M2),
@@ -165,9 +177,9 @@ def tile_list_meet_plain_levelled_steps_kernel(
                     stop=True,
                 )
                 first = LEAD + h * HALF
-                nc.scalar.copy(out=scores[:, a, first : first + HALF], in_=bank[:])
-                step = sb.tile([P, HALF], F32, name="step%d%d" % (a, h), align_bytes=64)
-                nc.vector.tensor_tensor(step[:], bank[:], scores[:, a, first - 1 : first - 1 + HALF], ALU.subtract)
+                nc.scalar.copy(out=scores[:, a, first : first + HALF], in_=a0[:])
+                change = sb.tile([P, HALF], F32, name="change%d%d" % (a, h), align_bytes=64)
+                nc.vector.tensor_tensor(change[:], a0[:], scores[:, a, first - 1 : first - 1 + HALF], ALU.subtract)
                 result = sb.tile([P, HALF], F32, name="result%d%d" % (a, h), align_bytes=64)
-                nc.scalar.activation(result[:], step[:], ACT.Abs, scale=0.04)
+                nc.scalar.activation(result[:], change[:], ACT.Abs, scale=FACTOR)
                 nc.sync.dma_start(out=out[a * P : (a + 1) * P, h * HALF : (h + 1) * HALF], in_=result[:])

from contextlib import ExitStack

import concourse.mybir as mybir

K, T, J, I, R = 512, 512, 256, 256, 512
FLOPS = 2 * K * R * J + 2 * K * R * I + 2 * R * J * I

F32 = mybir.dt.float32
BF16 = mybir.dt.bfloat16
I32 = mybir.dt.int32
U32 = mybir.dt.uint32
U16 = mybir.dt.uint16
U8 = mybir.dt.uint8
E2M1 = mybir.dt.float4_e2m1fn_x4
E4M3 = mybir.dt.float8_e4m3fn_x4
E5M2 = mybir.dt.float8_e5m2_x4
ALU = mybir.AluOpType
ACT = mybir.ActivationFunctionType

P = 128
PACK = 4
QUADRANTS = 4
RUN = 8
GROUP = 16
HALF = 128
BUNDLE = 8
LEAD = 4
FACTOR = 0.04


def load_scale_rows(queues, plane, scales):
    rows = scales[0].bitcast(I32)
    for q in range(QUADRANTS):
        queues[q].dma_start(out=plane[:].bitcast(I32)[32 * q : 32 * q + 4, :], in_=rows[4 * q : 4 * q + 4, :])


def load_weight_words(nc, raw, words):
    nc.sync.dma_start(out=raw[:].bitcast(I32), in_=words[0].rearrange("p n t -> p (n t)").bitcast(I32))


def deal_weight(nc, words, plane, raw_words, raw_plane):
    for dealt, raw, run in (
        (words[:], raw_words[:], RUN),
        (plane[:].bitcast(U32), raw_plane[:].bitcast(U32), RUN // 4),
    ):
        nc.scalar.copy(
            out=dealt.rearrange("p (t b u) -> p t b u", t=PACK, u=run),
            in_=raw.rearrange("p (b t u) -> p t b u", t=PACK, u=run),
        )


def first_stage(nc, bank, w_words, w_plane, w_format, picked_words, picked_plane):
    for t in range(PACK):
        cols = slice(t * P, (t + 1) * P)
        nc.tensor.matmul_mx(
            out=bank[:, t, :],
            lhsT=w_words[:, cols].bitcast(w_format),
            lhsT_scale=w_plane[:, cols],
            rhs=picked_words.bitcast(E2M1),
            rhs_scale=picked_plane,
            start=True,
            stop=True,
        )


def quantise(nc, pool, name, values):
    words = pool.tile([P, HALF], U32, name=name + "_words", align_bytes=64)
    plane = pool.tile([P, HALF], U8, name=name + "_plane", align_bytes=64)
    nc.vector.quantize_mx(out=words[:].bitcast(E5M2), scales=plane[:], in_=values[:].rearrange("p n t -> p (n t)"))
    return words, plane


def tile_list_meet_plain_levelled_steps_kernel(
    tc, xt_words, xt_scales, wa_words, wa_scales, wb_words, wb_scales, offs, offs2, out
):
    nc = tc.nc
    with ExitStack() as ctx:
        sb = ctx.enter_context(tc.tile_pool(name="sb", bufs=1))
        ps = ctx.enter_context(tc.psum_pool(name="ps", bufs=1))

        rows_list = sb.tile([P, J // GROUP], U16, name="rows_list")
        cols_list = sb.tile([P, I // GROUP], U16, name="cols_list")
        x_words = sb.tile([P, T], U16, name="x_words", align_bytes=64)
        x_plane = sb.tile([P, T], U8, name="x_plane", align_bytes=64)
        wa_raw = sb.tile([P, R], U32, name="wa_raw", align_bytes=64)
        wb_raw = sb.tile([P, R], U32, name="wb_raw", align_bytes=64)
        wa_raw_plane = sb.tile([P, R], U8, name="wa_raw_plane", align_bytes=64)
        wb_raw_plane = sb.tile([P, R], U8, name="wb_raw_plane", align_bytes=64)
        wa = sb.tile([P, R], U32, name="wa", align_bytes=64)
        wb = sb.tile([P, R], U32, name="wb", align_bytes=64)
        wa_plane = sb.tile([P, R], U8, name="wa_plane", align_bytes=64)
        wb_plane = sb.tile([P, R], U8, name="wb_plane", align_bytes=64)
        scores = sb.tile([P, 2, LEAD + I], F32, name="scores", align_bytes=64)

        zero = sb.tile([P, 2, 1], F32, name="zero", align_bytes=64)
        nc.gpsimd.memset(x_plane[:].bitcast(I32), 0)
        nc.gpsimd.memset(wb_raw_plane[:].bitcast(I32), 0)
        nc.gpsimd.memset(zero[:], 0.0)
        nc.vector.memset(wa_raw_plane[:].bitcast(I32), 0)

        nc.sync.dma_start(cols_list[:], offs2)
        nc.sync.dma_start(out=x_words[:].bitcast(I32), in_=xt_words[0].bitcast(I32))
        nc.sync.dma_start(rows_list[:], offs)
        load_weight_words(nc, wb_raw, wb_words)
        load_scale_rows([nc.scalar] * QUADRANTS, x_plane, xt_scales)
        nc.scalar.activation(scores[:, :, LEAD - 1 : LEAD], zero[:], ACT.Copy)
        load_scale_rows([nc.gpsimd, nc.sync, nc.sync, nc.sync], wb_raw_plane, wb_scales)
        load_weight_words(nc, wa_raw, wa_words)
        load_scale_rows([nc.sync] * QUADRANTS, wa_raw_plane, wa_scales)

        deal_weight(nc, wb, wb_plane, wb_raw, wb_raw_plane)

        zb = []
        for h in range(2):
            entries = cols_list[:, h * HALF // GROUP : (h + 1) * HALF // GROUP]
            xb_words = sb.tile([P, HALF], U16, name="xb_words%d" % h, align_bytes=64)
            xb_plane = sb.tile([P, HALF], U8, name="xb_plane%d" % h, align_bytes=64)
            nc.vector.tensor_copy(xb_words[:], x_words[:].indirect(entries))
            nc.vector.tensor_copy(xb_plane[:], x_plane[:].indirect(entries))
            zb_half = ps.tile([P, PACK, HALF], F32, name="zb%d" % h)
            first_stage(nc, zb_half, wb, wb_plane, E4M3, xb_words[:], xb_plane[:])
            zb.append(zb_half)

        xa_words = sb.tile([P, J], U16, name="xa_words", align_bytes=64)
        xa_plane = sb.tile([P, J], U8, name="xa_plane", align_bytes=64)
        nc.vector.tensor_copy(xa_words[:], x_words[:].indirect(rows_list[:]))
        nc.vector.tensor_copy(xa_plane[:], x_plane[:].indirect(rows_list[:]))

        means = []
        for h in range(2):
            sums = sb.tile([P, HALF // BUNDLE, PACK], F32, name="sums%d" % h, align_bytes=64)
            nc.vector.tensor_reduce(
                out=sums[:],
                in_=zb[h][:].rearrange("p t (g e) -> p g t e", e=BUNDLE),
                axis=mybir.AxisListType.X,
                op=ALU.add,
            )
            mean = sb.tile([P, HALF // BUNDLE, PACK], F32, name="mean%d" % h, align_bytes=64)
            nc.gpsimd.tensor_scalar(mean[:], sums[:], 1.0 / BUNDLE, 0.0, ALU.mult, ALU.add)
            means.append(mean)

        deal_weight(nc, wa, wa_plane, wa_raw, wa_raw_plane)
        ha = []
        for h in range(2):
            cols = slice(h * HALF, (h + 1) * HALF)
            za_half = ps.tile([P, PACK, HALF], F32, name="za%d" % h)
            first_stage(nc, za_half, wa, wa_plane, E5M2, xa_words[:, cols], xa_plane[:, cols])
            ha_half = sb.tile([P, HALF, PACK], BF16, name="ha%d" % h, align_bytes=64)
            nc.scalar.activation(ha_half[:], za_half[:].rearrange("p t n -> p n t"), ACT.Relu)
            ha.append(ha_half)

        hb = []
        for h in range(2):
            hb_half = sb.tile([P, HALF, PACK], BF16, name="hb%d" % h, align_bytes=64)
            nc.vector.tensor_tensor(
                hb_half[:].rearrange("p (g e) t -> p g e t", e=BUNDLE),
                zb[h][:].rearrange("p t (g e) -> p g e t", e=BUNDLE),
                means[h][:].unsqueeze(2).to_broadcast([P, HALF // BUNDLE, BUNDLE, PACK]),
                ALU.subtract,
            )
            hb.append(hb_half)

        haq_first = quantise(nc, sb, "ha0", ha[0])
        hbq = [quantise(nc, sb, "hb0", hb[0]), quantise(nc, sb, "hb1", hb[1])]
        haq = [haq_first, quantise(nc, sb, "ha1", ha[1])]

        for a in range(2):
            for h in range(2):
                a0 = ps.tile([P, HALF], F32, name="a0_%d%d" % (a, h))
                nc.tensor.matmul_mx(
                    out=a0[:],
                    lhsT=haq[a][0][:].bitcast(E5M2),
                    lhsT_scale=haq[a][1][:],
                    rhs=hbq[h][0][:].bitcast(E5M2),
                    rhs_scale=hbq[h][1][:],
                    start=True,
                    stop=True,
                )
                first = LEAD + h * HALF
                nc.scalar.copy(out=scores[:, a, first : first + HALF], in_=a0[:])
                change = sb.tile([P, HALF], F32, name="change%d%d" % (a, h), align_bytes=64)
                nc.vector.tensor_tensor(change[:], a0[:], scores[:, a, first - 1 : first - 1 + HALF], ALU.subtract)
                result = sb.tile([P, HALF], F32, name="result%d%d" % (a, h), align_bytes=64)
                nc.scalar.activation(result[:], change[:], ACT.Abs, scale=FACTOR)
                nc.sync.dma_start(out=out[a * P : (a + 1) * P, h * HALF : (h + 1) * HALF], in_=result[:])
